import numpy as np
import ml_dtypes


def mxq(x, axis, fmt="e4m3"):
    dtype, down = {"e4m3": (ml_dtypes.float8_e4m3fn, 7), "e5m2": (ml_dtypes.float8_e5m2, 14)}[fmt]
    v = np.moveaxis(np.asarray(x, np.float32).astype(ml_dtypes.bfloat16).astype(np.float64), axis, -1)
    blocks = v.reshape(v.shape[:-1] + (-1, 32))
    amax = np.abs(blocks).max(-1, keepdims=True)
    byte = np.maximum(np.where(amax > 0, np.frexp(amax)[1] - 1 + 127, 0) - down, 1)
    scale = np.exp2(byte - 127.0)
    codes = (blocks / scale).astype(np.float32).astype(dtype).astype(np.float64)
    return np.moveaxis((codes * scale).reshape(v.shape), -1, axis)


WIDE = False


def mx_kscale(k):
    if not WIDE:
        return np.ones(k)
    levels = np.array([10, -10, 5, -5, 0])
    if k % 512:
        return np.exp2(np.random.permutation(np.resize(levels, k // 32))).repeat(32)
    a = np.empty((k // 512, 16))
    for p in range(k // 512):
        a[p, :8] = np.random.permutation(np.resize(levels, 8))
        for g in range(8):
            far = levels[np.abs(levels - a[p, g]) >= 10]
            a[p, g + 8] = far[np.random.randint(len(far))]
    return np.exp2(a.ravel()).repeat(32)


def f64(x):
    return np.asarray(x).astype(np.float64)


def striped(idx):
    return np.tile(np.asarray(idx).reshape(-1, 16).T, (8, 1)).astype(np.uint16)


def unstriped(offs):
    return offs[:16].T.reshape(-1).astype(np.int64)


def striped8(idx):
    return np.asarray(idx).reshape(8, -1, 16).transpose(0, 2, 1).reshape(128, -1).astype(np.uint16)


def unstriped8(offs):
    return offs.reshape(8, 16, -1).transpose(0, 2, 1).reshape(8, -1).astype(np.int64)


def pick8(x, idx, run):
    r = np.arange(len(x))
    return x[r[:, None], idx[r % (8 * run) // run]]


E2M1 = np.array([0.0, 0.5, 1.0, 1.5, 2.0, 3.0, 4.0, 6.0, -0.0, -0.5, -1.0, -1.5, -2.0, -3.0, -4.0, -6.0])


def pack_weight(w, fmt):
    k, n = w.shape
    w = f64(np.asarray(w, np.float32).astype(ml_dtypes.bfloat16)).reshape(k // 32, 32, n)
    amax = np.abs(w).max(1)
    if fmt == "e4m3":
        byte = np.frexp(amax)[1] - 1 + 127 - 7
    else:
        mant, ex = np.frexp(amax / 6.0)
        byte = np.where(mant > 0.5, ex, ex - 1) + 127
    byte = np.clip(np.where(amax > 0, byte, 1), 1, 254)
    scaled = (w * np.exp2(127.0 - byte)[:, None, :]).reshape(k, n).astype(np.float32)
    by_word = np.ascontiguousarray(scaled.reshape(k // 512, 128, 4, n).transpose(0, 1, 3, 2))
    if fmt == "e4m3":
        words = by_word.astype(ml_dtypes.float8_e4m3fn).view(np.uint8)
    else:
        c = by_word.astype(ml_dtypes.float4_e2m1fn).view(np.uint8) & 0xF
        words = (c[..., 0::2] | (c[..., 1::2] << 4)).reshape(k // 512, 128, 2 * n)
    return np.ascontiguousarray(words), np.ascontiguousarray(byte.astype(np.uint8).reshape(k // 512, 16, n))


def unpack_weight(words, scales, fmt):
    g, _, n = scales.shape
    words = np.ascontiguousarray(words).reshape(g, 128, n, -1)
    if fmt == "e4m3":
        vals = words.view(ml_dtypes.float8_e4m3fn).astype(np.float64)
    else:
        nib = np.empty((g, 128, n, 4), np.uint8)
        nib[..., 0::2] = words & 0xF
        nib[..., 1::2] = words >> 4
        vals = E2M1[nib]
    vals = vals * np.repeat(np.exp2(scales.astype(np.float64) - 127.0), 8, axis=1)[..., None]
    return vals.transpose(0, 1, 3, 2).reshape(g * 512, n)


K, J, R, T, U, F, C, O, S, N, Z = 512, 256, 512, 1024, 512, 1024, 512, 128, 256, 256, 1024


def setup_inputs():
    n = np.random.standard_normal
    idx = np.stack([np.random.permutation(T)[:U] for _ in range(8)])
    idx2 = np.random.permutation(F)[:R]
    idx3 = np.stack([np.random.permutation(C)[:J] for _ in range(8)])
    idx4 = np.stack([np.random.permutation(C)[:S] for _ in range(8)])
    idx5 = np.random.permutation(C)[:S]
    idx6 = np.stack([np.random.permutation(S)[:O] for _ in range(8)])
    idx7 = np.random.permutation(Z)[:N]
    fk = mx_kscale(K)
    fr = mx_kscale(R)
    tr = np.ones(F)
    tr[idx2] = fr
    wtp = pack_weight(n((K, F)) * 1 / np.sqrt(K) / fk[:, None] * tr, "e4m3")
    vsp = pack_weight(n((R, Z)) * 1 / np.sqrt(R) / fr[:, None], "e2m1")
    return {
        "ta": (np.random.randint(-7, 8, (K, T)).astype(np.float64)).astype(np.float32),
        "ga": ((np.random.randint(8, 25, (K, 1)) / 64.0) * fk[:, None]).astype(np.float32),
        "wt_words": wtp[0],
        "wt_scales": wtp[1],
        "sa": (np.random.uniform(0.5, 1.6, (R, 1))).astype(np.float32),
        "sb": (np.random.uniform(0.5, 1.6, (R, 1))).astype(np.float32),
        "sd": (np.random.uniform(0.5, 1.6, (R, 1))).astype(np.float32),
        "vs_words": vsp[0],
        "vs_scales": vsp[1],
        "offs": striped8(idx),
        "offs2": striped(idx2),
        "offs3": striped8(idx3),
        "offs4": striped8(idx4),
        "offs5": striped(idx5),
        "offs6": striped8(idx6),
        "offs7": striped(idx7),
    }


def reference(ta, ga, wt_words, wt_scales, sa, sb, sd, vs_words, vs_scales, offs, offs2, offs3, offs4, offs5, offs6, offs7):
    idx = unstriped8(offs)
    idx2 = unstriped(offs2)
    idx3 = unstriped8(offs3)
    idx4 = unstriped8(offs4)
    idx5 = unstriped(offs5)
    idx6 = unstriped8(offs6)
    idx7 = unstriped(offs7)
    wtu = unpack_weight(wt_words, wt_scales, "e4m3")
    vsu = unpack_weight(vs_words, vs_scales, "e2m1")
    xcd = pick8(f64(ta), idx, 64) * f64(ga)
    xc = xcd.reshape(K, J, U // J).max(axis=2)
    wtidx2g = wtu[:, idx2]
    xcq = mxq(xc, 0, "e4m3")
    a = wtidx2g.T @ xcq
    pw = np.zeros((R, C))
    pw[np.arange(R)[:, None], idx3[np.arange(R) % 512 // 64]] = a
    pg = np.maximum(pick8(pw, idx4, 64) * f64(sa), pw[:, idx5] * f64(sb))
    hid = pick8(pg, idx6, 64) * f64(sd)
    vsidx7g = vsu[:, idx7]
    hidq = mxq(hid, 0, "e4m3")
    y = vsidx7g.T @ hidq
    return y

@@ -1,0 +1,202 @@
+from contextlib import ExitStack
+
+import concourse.mybir as mybir
+
+K, J, R, T, U, F, C, O, S, N, Z = 512, 256, 512, 1024, 512, 1024, 512, 128, 256, 256, 1024
+FLOPS = 2 * K * R * J + 2 * R * N * O
+
+F32 = mybir.dt.float32
+BF16 = mybir.dt.bfloat16
+I32 = mybir.dt.int32
+U32 = mybir.dt.uint32
+U16 = mybir.dt.uint16
+U8 = mybir.dt.uint8
+FP8X4 = mybir.dt.float8_e4m3fn_x4
+FP4X4 = mybir.dt.float4_e2m1fn_x4
+COPY = mybir.ActivationFunctionType.Copy
+MAX = mybir.AluOpType.max
+
+P = 128
+PACK = 4
+QUAD = 32
+HALVES = 2
+JH = J // HALVES
+UH = U // HALVES
+
+
+def tile_picked_codepool_store_one_ladder_store_plain_kernel(
+    tc, ta, ga, wt_words, wt_scales, sa, sb, sd, vs_words, vs_scales,
+    offs, offs2, offs3, offs4, offs5, offs6, offs7, out,
+):
+    nc = tc.nc
+    with ExitStack() as ctx:
+        pool = ctx.enter_context(tc.tile_pool(name="sbuf", bufs=1))
+        psum = ctx.enter_context(tc.psum_pool(name="psum", bufs=1))
+
+        def load_list(name, src):
+            tile = pool.tile([P, src.shape[1]], U16, name=name)
+            nc.sync.dma_start(tile[:], src)
+            return tile
+
+        def load_column(name, src, queue):
+            tile = pool.tile([P, PACK], F32, name=name)
+            queue.dma_start(tile[:], src.rearrange("(p t) o -> p (t o)", t=PACK))
+            return tile
+
+        def load_scale_rows(name, src):
+            tile = pool.tile([PACK, PACK, src.shape[2] // 4], I32, name=name)
+            nc.scalar.dma_start(tile[:], src[0].bitcast(I32).rearrange("(q r) c -> r q c", r=PACK))
+            return tile
+
+        def spread_scale_rows(name, rows):
+            tile = pool.tile([P, rows.shape[2]], I32, name=name)
+            nc.vector.memset(tile[:], 0)
+            for q in range(PACK):
+                nc.vector.tensor_copy(tile[QUAD * q : QUAD * q + PACK, :], rows[:, q, :])
+            return tile
+
+        ta_rows = ta.rearrange("(p t) c -> t p c", t=PACK)
+        ta_sb = [pool.tile([P, T], F32, name=f"ta{t}") for t in range(PACK)]
+
+        ga_sb = load_column("ga", ga, nc.scalar)
+        nc.sync.dma_start(ta_sb[0][:], ta_rows[0])
+        wt_rows = load_scale_rows("wt_rows", wt_scales)
+        list1 = load_list("list1", offs)
+        list2 = load_list("list2", offs2)
+        for t in range(1, PACK - 1):
+            nc.sync.dma_start(ta_sb[t][:], ta_rows[t])
+        wt_all = pool.tile([P, F], I32, name="wt_all")
+        nc.sync.dma_start(wt_all[:], wt_words[0].rearrange("p n t -> p (n t)").bitcast(I32))
+        nc.sync.dma_start(ta_sb[PACK - 1][:], ta_rows[PACK - 1])
+        list3 = load_list("list3", offs3)
+        list4 = load_list("list4", offs4)
+        list5 = load_list("list5", offs5)
+        sa_sb = load_column("sa", sa, nc.sync)
+        sb_sb = load_column("sb", sb, nc.sync)
+        list6 = load_list("list6", offs6)
+        sd_sb = load_column("sd", sd, nc.sync)
+        list7 = load_list("list7", offs7)
+        vs_all = pool.tile([P, 2 * Z], U8, name="vs_all")
+        nc.sync.dma_start(vs_all[:].bitcast(I32), vs_words[0].bitcast(I32))
+        vs_plane = pool.tile([P, Z // 4], I32, name="vs_plane")
+        nc.gpsimd.memset(vs_plane[:], 0)
+        for q in range(PACK):
+            nc.sync.dma_start(
+                vs_plane[QUAD * q : QUAD * q + PACK, :], vs_scales[0, PACK * q : PACK * (q + 1), :].bitcast(I32)
+            )
+
+        pw = [pool.tile([P, C], F32, name=f"pw{t}") for t in range(PACK)]
+        for t in range(PACK):
+            nc.gpsimd.memset(pw[t][:], 0.0)
+
+        wt_plane = spread_scale_rows("wt_plane", wt_rows)
+        wt_sc_list = pool.tile([P, R], U8, name="wt_sc_list")
+        nc.vector.tensor_copy(wt_sc_list[:], wt_plane[:].bitcast(U8).indirect(list2[:]))
+        wt_sc = pool.tile([P, PACK, P], U8, name="wt_sc", align_bytes=64)
+        nc.vector.tensor_copy(
+            wt_sc[:].rearrange("p t (c i) -> p c t i", i=16),
+            wt_sc_list[:].rearrange("p (c i t) -> p c t i", i=16, t=PACK),
+        )
+        wt_list = pool.tile([P, R], U32, name="wt_list")
+        nc.vector.tensor_copy(wt_list[:], wt_all[:].bitcast(U32).indirect(list2[:]))
+        wt_q = pool.tile([P, PACK, P], U32, name="wt_q", align_bytes=64)
+        nc.vector.tensor_copy(
+            wt_q[:].rearrange("p t (c i) -> p c t i", i=4),
+            wt_list[:].rearrange("p (c i t) -> p c t i", i=4, t=PACK),
+        )
+
+        picks = [pool.tile([P, PACK, UH], F32, name=f"picks{h}") for h in range(HALVES)]
+        for h in range(HALVES):
+            for t in range(PACK):
+                nc.scalar.activation(
+                    out=picks[h][:, t, :],
+                    in_=ta_sb[t][:].indirect(list1[:, h * UH // 16 : (h + 1) * UH // 16]),
+                    func=COPY,
+                    scale=ga_sb[:, t : t + 1],
+                )
+        a_first = pool.tile([P, J], F32, name="a_first")
+        a_rest = pool.tile([P, PACK - 1, J], F32, name="a_rest")
+        first = []
+        rest = []
+        for h in range(HALVES):
+            xc = pool.tile([P, JH, PACK], BF16, name=f"xc{h}", align_bytes=64)
+            nc.vector.tensor_tensor(
+                xc[:].rearrange("p (c i) t -> p c t i", i=2),
+                picks[h][:, :, 0::2].rearrange("p t (c i) -> p c t i", i=2),
+                picks[h][:, :, 1::2].rearrange("p t (c i) -> p c t i", i=2),
+                MAX,
+            )
+            xc_q = pool.tile([P, JH], U32, name=f"xc_q{h}", align_bytes=64)
+            xc_sc = pool.tile([P, JH], U8, name=f"xc_sc{h}", align_bytes=64)
+            nc.vector.quantize_mx(
+                out=xc_q[:].bitcast(FP8X4), scales=xc_sc[:], in_=xc[:].rearrange("p j t -> p (j t)")
+            )
+            first.append(psum.tile([P, JH], F32, name=f"acc_first{h}"))
+            rest.append(psum.tile([P, PACK - 1, JH], F32, name=f"acc_rest{h}"))
+            for t in range(PACK):
+                nc.tensor.matmul_mx(
+                    out=first[h][:] if t == 0 else rest[h][:, t - 1, :],
+                    lhsT=wt_q[:, t, :].bitcast(FP8X4),
+                    lhsT_scale=wt_sc[:, t, :],
+                    rhs=xc_q[:].bitcast(FP8X4),
+                    rhs_scale=xc_sc[:],
+                    start=True,
+                    stop=True,
+                )
+        for h in range(HALVES):
+            nc.scalar.copy(a_first[:, h * JH : (h + 1) * JH], first[h][:])
+        for h in range(HALVES):
+            nc.scalar.copy(a_rest[:, :, h * JH : (h + 1) * JH], rest[h][:])
+
+        hid = pool.tile([P, PACK, O], BF16, name="hid")
+        by4 = [pool.tile([P, S], F32, name=f"by4_{t}", tag=f"by4_{t}", align_bytes=64) for t in range(PACK)]
+        by5 = [pool.tile([P, S], F32, name=f"by5_{t}") for t in range(PACK)]
+        pg = [pool.tile([P, S], F32, name=f"pg{t}") for t in range(PACK)]
+
+        for h in range(HALVES):
+            nc.vector.tensor_copy(
+                pw[0][:].indirect(list3[:, h * JH // 16 : (h + 1) * JH // 16]),
+                a_first[:, h * JH : (h + 1) * JH],
+            )
+        for t in range(1, PACK):
+            nc.vector.tensor_copy(pw[t][:].indirect(list3[:]), a_rest[:, t - 1, :])
+        for t in range(PACK):
+            nc.scalar.activation(out=by4[t][:], in_=pw[t][:].indirect(list4[:]), func=COPY, scale=sa_sb[:, t : t + 1])
+            nc.scalar.activation(out=by5[t][:], in_=pw[t][:].indirect(list5[:]), func=COPY, scale=sb_sb[:, t : t + 1])
+        for t in range(PACK):
+            nc.vector.tensor_tensor(pg[t][:], by4[t][:], by5[t][:], MAX)
+        vs_sc = pool.tile([P, N], U8, name="vs_sc", tag=f"by4_{PACK - 2}", align_bytes=64)
+        nc.vector.tensor_copy(vs_sc[:], vs_plane[:].bitcast(U8).indirect(list7[:]))
+        vs_q = pool.tile([P, 2 * N], U8, name="vs_q", tag=f"by4_{PACK - 1}", align_bytes=64)
+        nc.vector.tensor_copy(vs_q[:].bitcast(U16), vs_all[:].bitcast(U16).indirect(list7[:]))
+        for t in range(PACK):
+            nc.scalar.activation(out=hid[:, t, :], in_=pg[t][:].indirect(list6[:]), func=COPY, scale=sd_sb[:, t : t + 1])
+
+        hid_x4 = pool.tile([P, O, PACK], BF16, name="hid_x4", align_bytes=64)
+        nc.vector.tensor_copy(
+            hid_x4[:].rearrange("p (c i) t -> p c t i", i=4),
+            hid[:].rearrange("p t (c i) -> p c t i", i=4),
+        )
+        hid_q = pool.tile([P, O], U32, name="hid_q", align_bytes=64)
+        hid_sc = pool.tile([P, O], U8, name="hid_sc", align_bytes=64)
+        nc.vector.quantize_mx(
+            out=hid_q[:].bitcast(FP8X4), scales=hid_sc[:], in_=hid_x4[:].rearrange("p o t -> p (o t)")
+        )
+        for b in range(N // P):
+            y = psum.tile([P, O], F32, name=f"y{b}")
+            nc.tensor.matmul_mx(
+                out=y[:],
+                lhsT=vs_q[:, 2 * P * b : 2 * P * (b + 1)].bitcast(FP4X4),
+                lhsT_scale=vs_sc[:, P * b : P * (b + 1)],
+                rhs=hid_q[:].bitcast(FP8X4),
+                rhs_scale=hid_sc[:],
+                start=True,
+                stop=True,
+            )
+            y_sb = pool.tile([P, O], F32, name=f"y_sb{b}")
+            if b == 0:
+                nc.scalar.copy(y_sb[:], y[:])
+                nc.scalar.dma_start(out[P * b : P * (b + 1), :], y_sb[:])
+            else:
+                nc.vector.tensor_copy(y_sb[:], y[:])
+                nc.sync.dma_start(out[P * b : P * (b + 1), :], y_sb[:])

@@ -78,8 +78,8 @@ def tile_picked_codepool_store_one_ladder_store_plain_kernel(
         list7 = load_list("list7", offs7)
         vs_all = pool.tile([P, 2 * Z], U8, name="vs_all")
         nc.sync.dma_start(vs_all[:].bitcast(I32), vs_words[0].bitcast(I32))
-        vs_plane = pool.tile([P, Z // 4], I32, name="vs_plane")
-        nc.gpsimd.memset(vs_plane[:], 0)
+        vs_plane = pool.tile([P, Z // 4], I32, name="vs_plane", tag="vs_plane_then_pg")
+        nc.vector.memset(vs_plane[:], 0)
         for q in range(PACK):
             nc.sync.dma_start(
                 vs_plane[QUAD * q : QUAD * q + PACK, :], vs_scales[0, PACK * q : PACK * (q + 1), :].bitcast(I32)
@@ -87,7 +87,7 @@ def tile_picked_codepool_store_one_ladder_store_plain_kernel(
 
         pw = [pool.tile([P, C], F32, name=f"pw{t}") for t in range(PACK)]
         for t in range(PACK):
-            nc.gpsimd.memset(pw[t][:], 0.0)
+            nc.vector.memset(pw[t][:], 0.0)
 
         wt_plane = spread_scale_rows("wt_plane", wt_rows)
         wt_sc_list = pool.tile([P, R], U8, name="wt_sc_list")
@@ -151,7 +151,6 @@ def tile_picked_codepool_store_one_ladder_store_plain_kernel(
         hid = pool.tile([P, PACK, O], BF16, name="hid")
         by4 = [pool.tile([P, S], F32, name=f"by4_{t}", tag=f"by4_{t}", align_bytes=64) for t in range(PACK)]
         by5 = [pool.tile([P, S], F32, name=f"by5_{t}") for t in range(PACK)]
-        pg = [pool.tile([P, S], F32, name=f"pg{t}") for t in range(PACK)]
 
         for h in range(HALVES):
             nc.vector.tensor_copy(
@@ -163,10 +162,13 @@ def tile_picked_codepool_store_one_ladder_store_plain_kernel(
         for t in range(PACK):
             nc.scalar.activation(out=by4[t][:], in_=pw[t][:].indirect(list4[:]), func=COPY, scale=sa_sb[:, t : t + 1])
             nc.scalar.activation(out=by5[t][:], in_=pw[t][:].indirect(list5[:]), func=COPY, scale=sb_sb[:, t : t + 1])
-        for t in range(PACK):
+        pg = [pool.tile([P, S], F32, name=f"pg{t}") for t in range(PACK - 1)]
+        for t in range(PACK - 1):
             nc.vector.tensor_tensor(pg[t][:], by4[t][:], by5[t][:], MAX)
         vs_sc = pool.tile([P, N], U8, name="vs_sc", tag=f"by4_{PACK - 2}", align_bytes=64)
         nc.vector.tensor_copy(vs_sc[:], vs_plane[:].bitcast(U8).indirect(list7[:]))
+        pg.append(pool.tile([P, S], F32, name="pg_last", tag="vs_plane_then_pg"))
+        nc.vector.tensor_tensor(pg[-1][:], by4[-1][:], by5[-1][:], MAX)
         vs_q = pool.tile([P, 2 * N], U8, name="vs_q", tag=f"by4_{PACK - 1}", align_bytes=64)
         nc.vector.tensor_copy(vs_q[:].bitcast(U16), vs_all[:].bitcast(U16).indirect(list7[:]))
         for t in range(PACK):

@@ -55,6 +55,11 @@ def tile_picked_codepool_store_one_ladder_store_plain_kernel(
                 nc.vector.tensor_copy(tile[QUAD * q : QUAD * q + PACK, :], rows[:, q, :])
             return tile
 
+        warm_in = pool.tile([P, 1], F32, name="warm_in")
+        warm_out = pool.tile([P, 1], F32, name="warm_out")
+        nc.vector.memset(warm_in[:], 0.0)
+        nc.scalar.activation(out=warm_out[:], in_=warm_in[:], func=COPY)
+
         ta_rows = ta.rearrange("(p t) c -> t p c", t=PACK)
         ta_sb = [pool.tile([P, T], F32, name=f"ta{t}") for t in range(PACK)]
 

@@ -45,7 +45,7 @@ def tile_picked_codepool_store_one_ladder_store_plain_kernel(
 
         def load_scale_rows(name, src):
             tile = pool.tile([PACK, PACK, src.shape[2] // 4], I32, name=name)
-            nc.scalar.dma_start(tile[:], src[0].bitcast(I32).rearrange("(q r) c -> r q c", r=PACK))
+            nc.sync.dma_start(tile[:], src[0].bitcast(I32).rearrange("(q r) c -> r q c", r=PACK))
             return tile
 
         def spread_scale_rows(name, rows):
@@ -65,9 +65,9 @@ def tile_picked_codepool_store_one_ladder_store_plain_kernel(
 
         ga_sb = load_column("ga", ga, nc.scalar)
         nc.sync.dma_start(ta_sb[0][:], ta_rows[0])
-        wt_rows = load_scale_rows("wt_rows", wt_scales)
         list1 = load_list("list1", offs)
         list2 = load_list("list2", offs2)
+        wt_rows = load_scale_rows("wt_rows", wt_scales)
         for t in range(1, PACK - 1):
             nc.sync.dma_start(ta_sb[t][:], ta_rows[t])
         wt_all = pool.tile([P, F], I32, name="wt_all")
@@ -110,12 +110,13 @@ def tile_picked_codepool_store_one_ladder_store_plain_kernel(
             wt_list[:].rearrange("p (c i t) -> p c t i", i=4, t=PACK),
         )
 
-        picks = [pool.tile([P, PACK, UH], F32, name=f"picks{h}") for h in range(HALVES)]
-        for h in range(HALVES):
-            for t in range(PACK):
+        picks = pool.tile([P, PACK, U], F32, name="picks")
+        for t in range(PACK):
+            step = UH if t == PACK - 1 else U
+            for u0 in range(0, U, step):
                 nc.scalar.activation(
-                    out=picks[h][:, t, :],
-                    in_=ta_sb[t][:].indirect(list1[:, h * UH // 16 : (h + 1) * UH // 16]),
+                    out=picks[:, t, u0 : u0 + step],
+                    in_=ta_sb[t][:].indirect(list1[:, u0 // 16 : (u0 + step) // 16]),
                     func=COPY,
                     scale=ga_sb[:, t : t + 1],
                 )
@@ -127,8 +128,8 @@ def tile_picked_codepool_store_one_ladder_store_plain_kernel(
             xc = pool.tile([P, JH, PACK], BF16, name=f"xc{h}", align_bytes=64)
             nc.vector.tensor_tensor(
                 xc[:].rearrange("p (c i) t -> p c t i", i=2),
-                picks[h][:, :, 0::2].rearrange("p t (c i) -> p c t i", i=2),
-                picks[h][:, :, 1::2].rearrange("p t (c i) -> p c t i", i=2),
+                picks[:, :, h * UH : (h + 1) * UH : 2].rearrange("p t (c i) -> p c t i", i=2),
+                picks[:, :, h * UH + 1 : (h + 1) * UH : 2].rearrange("p t (c i) -> p c t i", i=2),
                 MAX,
             )
             xc_q = pool.tile([P, JH], U32, name=f"xc_q{h}", align_bytes=64)

from contextlib import ExitStack

import concourse.mybir as mybir

K, J, R, T, U, F, C, O, S, N, Z = 512, 256, 512, 1024, 512, 1024, 512, 128, 256, 256, 1024
FLOPS = 2 * K * R * J + 2 * R * N * O

F32 = mybir.dt.float32
BF16 = mybir.dt.bfloat16
I32 = mybir.dt.int32
U32 = mybir.dt.uint32
U16 = mybir.dt.uint16
U8 = mybir.dt.uint8
FP8X4 = mybir.dt.float8_e4m3fn_x4
FP4X4 = mybir.dt.float4_e2m1fn_x4
COPY = mybir.ActivationFunctionType.Copy
MAX = mybir.AluOpType.max

P = 128
PACK = 4
QUAD = 32
HALVES = 2
JH = J // HALVES
UH = U // HALVES


def tile_picked_codepool_store_one_ladder_store_plain_kernel(
    tc, ta, ga, wt_words, wt_scales, sa, sb, sd, vs_words, vs_scales,
    offs, offs2, offs3, offs4, offs5, offs6, offs7, out,
):
    nc = tc.nc
    with ExitStack() as ctx:
        pool = ctx.enter_context(tc.tile_pool(name="sbuf", bufs=1))
        psum = ctx.enter_context(tc.psum_pool(name="psum", bufs=1))

        def load_list(name, src):
            tile = pool.tile([P, src.shape[1]], U16, name=name)
            nc.sync.dma_start(tile[:], src)
            return tile

        def load_column(name, src, queue):
            tile = pool.tile([P, PACK], F32, name=name)
            queue.dma_start(tile[:], src.rearrange("(p t) o -> p (t o)", t=PACK))
            return tile

        def load_scale_rows(name, src):
            tile = pool.tile([PACK, PACK, src.shape[2] // 4], I32, name=name)
            nc.sync.dma_start(tile[:], src[0].bitcast(I32).rearrange("(q r) c -> r q c", r=PACK))
            return tile

        def spread_scale_rows(name, rows):
            tile = pool.tile([P, rows.shape[2]], I32, name=name)
            nc.vector.memset(tile[:], 0)
            for q in range(PACK):
                nc.vector.tensor_copy(tile[QUAD * q : QUAD * q + PACK, :], rows[:, q, :])
            return tile

        warm_in = pool.tile([P, 1], F32, name="warm_in")
        warm_out = pool.tile([P, 1], F32, name="warm_out")
        nc.vector.memset(warm_in[:], 0.0)
        nc.scalar.activation(out=warm_out[:], in_=warm_in[:], func=COPY)

        ta_rows = ta.rearrange("(p t) c -> t p c", t=PACK)
        ta_sb = [pool.tile([P, T], F32, name=f"ta{t}") for t in range(PACK)]

        ga_sb = load_column("ga", ga, nc.scalar)
        nc.sync.dma_start(ta_sb[0][:], ta_rows[0])
        list1 = load_list("list1", offs)
        list2 = load_list("list2", offs2)
        wt_rows = load_scale_rows("wt_rows", wt_scales)
        for t in range(1, PACK - 1):
            nc.sync.dma_start(ta_sb[t][:], ta_rows[t])
        wt_all = pool.tile([P, F], I32, name="wt_all")
        nc.sync.dma_start(wt_all[:], wt_words[0].rearrange("p n t -> p (n t)").bitcast(I32))
        nc.sync.dma_start(ta_sb[PACK - 1][:], ta_rows[PACK - 1])
        list3 = load_list("list3", offs3)
        list4 = load_list("list4", offs4)
        list5 = load_list("list5", offs5)
        sa_sb = load_column("sa", sa, nc.sync)
        sb_sb = load_column("sb", sb, nc.sync)
        list6 = load_list("list6", offs6)
        sd_sb = load_column("sd", sd, nc.sync)
        list7 = load_list("list7", offs7)
        vs_all = pool.tile([P, 2 * Z], U8, name="vs_all")
        nc.sync.dma_start(vs_all[:].bitcast(I32), vs_words[0].bitcast(I32))
        vs_plane = pool.tile([P, Z // 4], I32, name="vs_plane", tag="vs_plane_then_pg")
        nc.vector.memset(vs_plane[:], 0)
        for q in range(PACK):
            nc.sync.dma_start(
                vs_plane[QUAD * q : QUAD * q + PACK, :], vs_scales[0, PACK * q : PACK * (q + 1), :].bitcast(I32)
            )

        pw = [pool.tile([P, C], F32, name=f"pw{t}") for t in range(PACK)]
        for t in range(PACK):
            nc.vector.memset(pw[t][:], 0.0)

        wt_plane = spread_scale_rows("wt_plane", wt_rows)
        wt_sc_list = pool.tile([P, R], U8, name="wt_sc_list")
        nc.vector.tensor_copy(wt_sc_list[:], wt_plane[:].bitcast(U8).indirect(list2[:]))
        wt_sc = pool.tile([P, PACK, P], U8, name="wt_sc", align_bytes=64)
        nc.vector.tensor_copy(
            wt_sc[:].rearrange("p t (c i) -> p c t i", i=16),
            wt_sc_list[:].rearrange("p (c i t) -> p c t i", i=16, t=PACK),
        )
        wt_list = pool.tile([P, R], U32, name="wt_list")
        nc.vector.tensor_copy(wt_list[:], wt_all[:].bitcast(U32).indirect(list2[:]))
        wt_q = pool.tile([P, PACK, P], U32, name="wt_q", align_bytes=64)
        nc.vector.tensor_copy(
            wt_q[:].rearrange("p t (c i) -> p c t i", i=4),
            wt_list[:].rearrange("p (c i t) -> p c t i", i=4, t=PACK),
        )

        picks = pool.tile([P, PACK, U], F32, name="picks")
        for t in range(PACK):
            step = UH if t == PACK - 1 else U
            for u0 in range(0, U, step):
                nc.scalar.activation(
                    out=picks[:, t, u0 : u0 + step],
                    in_=ta_sb[t][:].indirect(list1[:, u0 // 16 : (u0 + step) // 16]),
                    func=COPY,
                    scale=ga_sb[:, t : t + 1],
                )
        a_first = pool.tile([P, J], F32, name="a_first")
        a_rest = pool.tile([P, PACK - 1, J], F32, name="a_rest")
        first = []
        rest = []
        for h in range(HALVES):
            xc = pool.tile([P, JH, PACK], BF16, name=f"xc{h}", align_bytes=64)
            nc.vector.tensor_tensor(
                xc[:].rearrange("p (c i) t -> p c t i", i=2),
                picks[:, :, h * UH : (h + 1) * UH : 2].rearrange("p t (c i) -> p c t i", i=2),
                picks[:, :, h * UH + 1 : (h + 1) * UH : 2].rearrange("p t (c i) -> p c t i", i=2),
                MAX,
            )
            xc_q = pool.tile([P, JH], U32, name=f"xc_q{h}", align_bytes=64)
            xc_sc = pool.tile([P, JH], U8, name=f"xc_sc{h}", align_bytes=64)
            nc.vector.quantize_mx(
                out=xc_q[:].bitcast(FP8X4), scales=xc_sc[:], in_=xc[:].rearrange("p j t -> p (j t)")
            )
            first.append(psum.tile([P, JH], F32, name=f"acc_first{h}"))
            rest.append(psum.tile([P, PACK - 1, JH], F32, name=f"acc_rest{h}"))
            for t in range(PACK):
                nc.tensor.matmul_mx(
                    out=first[h][:] if t == 0 else rest[h][:, t - 1, :],
                    lhsT=wt_q[:, t, :].bitcast(FP8X4),
                    lhsT_scale=wt_sc[:, t, :],
                    rhs=xc_q[:].bitcast(FP8X4),
                    rhs_scale=xc_sc[:],
                    start=True,
                    stop=True,
                )
        for h in range(HALVES):
            nc.scalar.copy(a_first[:, h * JH : (h + 1) * JH], first[h][:])
        for h in range(HALVES):
            nc.scalar.copy(a_rest[:, :, h * JH : (h + 1) * JH], rest[h][:])

        hid = pool.tile([P, PACK, O], BF16, name="hid")
        by4 = [pool.tile([P, S], F32, name=f"by4_{t}", tag=f"by4_{t}", align_bytes=64) for t in range(PACK)]
        by5 = [pool.tile([P, S], F32, name=f"by5_{t}") for t in range(PACK)]

        for h in range(HALVES):
            nc.vector.tensor_copy(
                pw[0][:].indirect(list3[:, h * JH // 16 : (h + 1) * JH // 16]),
                a_first[:, h * JH : (h + 1) * JH],
            )
        for t in range(1, PACK):
            nc.vector.tensor_copy(pw[t][:].indirect(list3[:]), a_rest[:, t - 1, :])
        for t in range(PACK):
            nc.scalar.activation(out=by4[t][:], in_=pw[t][:].indirect(list4[:]), func=COPY, scale=sa_sb[:, t : t + 1])
            nc.scalar.activation(out=by5[t][:], in_=pw[t][:].indirect(list5[:]), func=COPY, scale=sb_sb[:, t : t + 1])
        pg = [pool.tile([P, S], F32, name=f"pg{t}") for t in range(PACK - 1)]
        for t in range(PACK - 1):
            nc.vector.tensor_tensor(pg[t][:], by4[t][:], by5[t][:], MAX)
        vs_sc = pool.tile([P, N], U8, name="vs_sc", tag=f"by4_{PACK - 2}", align_bytes=64)
        nc.vector.tensor_copy(vs_sc[:], vs_plane[:].bitcast(U8).indirect(list7[:]))
        pg.append(pool.tile([P, S], F32, name="pg_last", tag="vs_plane_then_pg"))
        nc.vector.tensor_tensor(pg[-1][:], by4[-1][:], by5[-1][:], MAX)
        vs_q = pool.tile([P, 2 * N], U8, name="vs_q", tag=f"by4_{PACK - 1}", align_bytes=64)
        nc.vector.tensor_copy(vs_q[:].bitcast(U16), vs_all[:].bitcast(U16).indirect(list7[:]))
        for t in range(PACK):
            nc.scalar.activation(out=hid[:, t, :], in_=pg[t][:].indirect(list6[:]), func=COPY, scale=sd_sb[:, t : t + 1])

        hid_x4 = pool.tile([P, O, PACK], BF16, name="hid_x4", align_bytes=64)
        nc.vector.tensor_copy(
            hid_x4[:].rearrange("p (c i) t -> p c t i", i=4),
            hid[:].rearrange("p t (c i) -> p c t i", i=4),
        )
        hid_q = pool.tile([P, O], U32, name="hid_q", align_bytes=64)
        hid_sc = pool.tile([P, O], U8, name="hid_sc", align_bytes=64)
        nc.vector.quantize_mx(
            out=hid_q[:].bitcast(FP8X4), scales=hid_sc[:], in_=hid_x4[:].rearrange("p o t -> p (o t)")
        )
        for b in range(N // P):
            y = psum.tile([P, O], F32, name=f"y{b}")
            nc.tensor.matmul_mx(
                out=y[:],
                lhsT=vs_q[:, 2 * P * b : 2 * P * (b + 1)].bitcast(FP4X4),
                lhsT_scale=vs_sc[:, P * b : P * (b + 1)],
                rhs=hid_q[:].bitcast(FP8X4),
                rhs_scale=hid_sc[:],
                start=True,
                stop=True,
            )
            y_sb = pool.tile([P, O], F32, name=f"y_sb{b}")
            if b == 0:
                nc.scalar.copy(y_sb[:], y[:])
                nc.scalar.dma_start(out[P * b : P * (b + 1), :], y_sb[:])
            else:
                nc.vector.tensor_copy(y_sb[:], y[:])
                nc.sync.dma_start(out[P * b : P * (b + 1), :], y_sb[:])
